import numpy as np
import ml_dtypes


def mxq(x, axis, fmt="e4m3"):
    dtype, down = {"e4m3": (ml_dtypes.float8_e4m3fn, 7), "e5m2": (ml_dtypes.float8_e5m2, 14)}[fmt]
    v = np.moveaxis(np.asarray(x, np.float32).astype(ml_dtypes.bfloat16).astype(np.float64), axis, -1)
    blocks = v.reshape(v.shape[:-1] + (-1, 32))
    amax = np.abs(blocks).max(-1, keepdims=True)
    byte = np.maximum(np.where(amax > 0, np.frexp(amax)[1] - 1 + 127, 0) - down, 1)
    scale = np.exp2(byte - 127.0)
    codes = (blocks / scale).astype(np.float32).astype(dtype).astype(np.float64)
    return np.moveaxis((codes * scale).reshape(v.shape), -1, axis)


WIDE = False


def mx_kscale(k):
    if not WIDE:
        return np.ones(k)
    levels = np.array([10, -10, 5, -5, 0])
    if k % 512:
        return np.exp2(np.random.permutation(np.resize(levels, k // 32))).repeat(32)
    a = np.empty((k // 512, 16))
    for p in range(k // 512):
        a[p, :8] = np.random.permutation(np.resize(levels, 8))
        for g in range(8):
            far = levels[np.abs(levels - a[p, g]) >= 10]
            a[p, g + 8] = far[np.random.randint(len(far))]
    return np.exp2(a.ravel()).repeat(32)


def f64(x):
    return np.asarray(x).astype(np.float64)


def striped(idx):
    return np.tile(idx.reshape(-1, 16).T, (8, 1)).astype(np.uint16)


def unstriped(offs):
    return offs[:16].T.reshape(-1).astype(np.int64)


def striped8(idx):
    return np.concatenate([x.reshape(-1, 16).T for x in idx]).astype(np.uint16)


def runs(offs, k):
    lists = np.stack([offs[16 * r : 16 * r + 16].T.reshape(-1) for r in range(8)]).astype(np.int64)
    return lists[np.arange(k) % 512 // 64]


def pack_weight(w):
    k, n = w.shape
    w = f64(np.asarray(w, np.float32).astype(ml_dtypes.bfloat16)).reshape(k // 32, 32, n)
    amax = np.abs(w).max(1)
    byte = np.clip(np.where(amax > 0, np.frexp(amax)[1] - 1 + 127 - 7, 1), 1, 254)
    scaled = (w * np.exp2(127.0 - byte)[:, None, :]).reshape(k, n).astype(np.float32)
    words = np.ascontiguousarray(scaled.reshape(k // 512, 128, 4, n).transpose(0, 1, 3, 2)).astype(ml_dtypes.float8_e4m3fn).view(np.uint8)
    return words, np.ascontiguousarray(byte.astype(np.uint8).reshape(k // 512, 16, n))


def unpack_weight(words, scales):
    g, p, n, _ = words.shape
    vals = np.ascontiguousarray(words).view(ml_dtypes.float8_e4m3fn).astype(np.float64) * np.repeat(np.exp2(scales.astype(np.float64) - 127.0), 8, axis=1)[..., None]
    return vals.transpose(0, 1, 3, 2).reshape(g * 512, n)


def sigmoid(v):
    return 1.0 / (1.0 + np.exp(-np.maximum(v, -700.0)))


K, T, S, N, G, H, W, U = 512, 1024, 256, 512, 2048, 512, 128, 512


def setup_inputs():
    n = np.random.standard_normal
    s = mx_kscale(K)[:, None]
    u = mx_kscale(K)
    packed_xT = pack_weight(n((K, T)) * s)
    packed_dT = pack_weight(n((K, G)) / s)
    packed_w1 = pack_weight(n((H, N)) / np.sqrt(2 * H) / u[:, None])
    packed_w2 = pack_weight(n((K, N)) / np.sqrt(2 * K) / s)
    perm = np.random.permutation(S)
    perm2 = np.random.permutation(S)
    perm3 = np.random.permutation(U)
    return {
        "x_words": packed_xT[0],
        "x_scales": packed_xT[1],
        "d_words": packed_dT[0],
        "d_scales": packed_dT[1],
        "sl": np.random.uniform(1.0, 2.0, (H, 1)).astype(np.float32),
        "th": (0.5 * n((H, 1))).astype(np.float32),
        "gn": (np.random.uniform(0.5, 1.5, (H, 1)) * u[:, None]).astype(np.float32),
        "w1_words": packed_w1[0],
        "w1_scales": packed_w1[1],
        "w2_words": packed_w2[0],
        "w2_scales": packed_w2[1],
        "offs": striped(np.random.permutation(T)[:S]),
        "ka": striped8(np.random.randint(0, G, (8, H))),
        "kb": striped8(np.random.randint(0, G, (8, H))),
        "n1": striped(perm[:W]),
        "n2": striped(perm[W:]),
        "n3": striped(perm2[:W]),
        "n4": striped(perm2[W:]),
        "n5": striped(np.random.permutation(S)),
        "hz": striped8(np.random.randint(0, T, (8, S))),
        "n6": striped(perm3[:S]),
        "n7": striped(perm3[S:]),
        "n8": striped(np.random.permutation(S)),
        "n9": striped(np.random.permutation(S)),
    }


def reference(x_words, x_scales, d_words, d_scales, sl, th, gn, w1_words, w1_scales, w2_words, w2_scales, offs, ka, kb, n1, n2, n3, n4, n5, hz, n6, n7, n8, n9):
    d_ka = unpack_weight(d_words, d_scales)[np.arange(K)[:, None], runs(ka, K)]
    xq = unpack_weight(x_words, x_scales)[:, unstriped(offs)]
    d_kb = unpack_weight(d_words, d_scales)[np.arange(K)[:, None], runs(kb, K)]
    h = 0.0625 * (d_ka.T @ xq + d_kb.T @ xq)
    pa = h[:, unstriped(n1)]
    pb = h[:, unstriped(n2)]
    rb = np.minimum(pa, pb)
    ra = np.maximum(pa, pb)
    ua = np.zeros((H, S))
    ua[:, unstriped(n3)] = ra
    ub = ua.copy()
    ub[:, unstriped(n4)] = rb
    sg = sigmoid(f64(sl) * (ub[:, unstriped(n5)] - f64(th)))
    z = f64(gn) * (ub * sg)
    x_hz = unpack_weight(x_words, x_scales)[np.arange(K)[:, None], runs(hz, K)]
    h2 = unpack_weight(w1_words, w1_scales).T @ mxq(z, 0, "e4m3") + unpack_weight(w2_words, w2_scales).T @ x_hz
    dn = h2 - h2[:, unstriped(n9)]
    up = np.maximum(h2, h2[:, unstriped(n8)])
    ph = np.zeros((N, U))
    ph[:, unstriped(n6)] = up
    out = ph.copy()
    out[:, unstriped(n7)] = dn
    return out

@@ -1,0 +1,252 @@
+from contextlib import ExitStack
+
+import concourse.mybir as mybir
+
+K, T, S, N, G, H, W, U = 512, 1024, 256, 512, 2048, 512, 128, 512
+FLOPS = 4 * 2 * 512 * 512 * 256
+
+F32 = mybir.dt.float32
+BF16 = mybir.dt.bfloat16
+I32 = mybir.dt.int32
+U32 = mybir.dt.uint32
+U16 = mybir.dt.uint16
+U8 = mybir.dt.uint8
+FP8X4 = mybir.dt.float8_e4m3fn_x4
+ALU = mybir.AluOpType
+ACT = mybir.ActivationFunctionType
+P = 128
+PACK = 4
+HALF = S // 2
+
+
+def tile_picked_atznheordpagdd_none_p_kernel(
+    tc, x_words, x_scales, d_words, d_scales, sl, th, gn, w1_words, w1_scales, w2_words, w2_scales,
+    offs, ka, kb, n1, n2, n3, n4, n5, hz, n6, n7, n8, n9, out,
+):
+    nc = tc.nc
+    with ExitStack() as ctx:
+        lists = ctx.enter_context(tc.tile_pool(name="lists", bufs=1))
+        sb = ctx.enter_context(tc.tile_pool(name="sb", bufs=1))
+        psum = ctx.enter_context(tc.psum_pool(name="psum", bufs=1))
+
+        def load_list(name, src):
+            tile = lists.tile(list(src.shape), U16, name=name)
+            nc.sync.dma_start(tile[:], src)
+            return tile
+
+        def load_words(name, src):
+            tile = sb.tile([P, src.shape[2]], U32, name=name, align_bytes=64)
+            nc.sync.dma_start(tile[:].bitcast(I32), src[0].rearrange("p n t -> p (n t)").bitcast(I32))
+            return tile
+
+        def zeroed_bytes(name, width):
+            tile = sb.tile([P, width], U8, name=name, align_bytes=64)
+            nc.vector.memset(tile[:].bitcast(I32), 0)
+            return tile
+
+        def gather_packed(dst, table, offsets):
+            nc.vector.tensor_copy(dst, table[:].indirect(offsets[:]))
+
+        def place_scale_rows(dst, src, queue):
+            for a in range(4):
+                queue.dma_start(dst[a:P:32, :].bitcast(I32), src[8 * a : P : 32, :].bitcast(I32))
+
+        def mx(acc, lw, ls, rw, rs, start, stop):
+            nc.tensor.matmul_mx(acc, lhsT=lw.bitcast(FP8X4), lhsT_scale=ls, rhs=rw.bitcast(FP8X4), rhs_scale=rs, start=start, stop=stop)
+
+        d_sc = zeroed_bytes("d_sc", G)
+        x_sc = zeroed_bytes("x_sc", T)
+        placed = zeroed_bytes("placed", 2 * H + S)
+        placed_hz = zeroed_bytes("placed_hz", S)
+        w_sc = zeroed_bytes("w_sc", 2 * N)
+
+        warm = sb.tile([P, 2], F32, name="warm")
+        nc.vector.memset(warm[:, 0:1], 0.0)
+        nc.scalar.activation(warm[:, 1:2], warm[:, 0:1], ACT.Sigmoid)
+        ka_t = load_list("ka_t", ka)
+        nc.sync.dma_start(d_sc[0:P:8, :].bitcast(I32), d_scales[0].bitcast(I32))
+        kb_t = load_list("kb_t", kb)
+        offs_t = load_list("offs_t", offs)
+        nc.sync.dma_start(x_sc[0:P:8, :].bitcast(I32), x_scales[0].bitcast(I32))
+        d_w = load_words("d_w", d_words)
+        x_w = load_words("x_w", x_words)
+
+        picked_sc = sb.tile([P, 2 * H + S], U8, name="picked_sc", align_bytes=64)
+        gather_packed(picked_sc[:, 0:H], d_sc, ka_t)
+        gather_packed(picked_sc[:, H : 2 * H], d_sc, kb_t)
+        gather_packed(picked_sc[:, 2 * H :], x_sc, offs_t)
+        place_scale_rows(placed, picked_sc, nc.scalar)
+
+        n1_t = load_list("n1_t", n1)
+        n2_t = load_list("n2_t", n2)
+        n3_t = load_list("n3_t", n3)
+        n4_t = load_list("n4_t", n4)
+        n5_t = load_list("n5_t", n5)
+        rowv = {}
+        for name, src in (("sl", sl), ("th", th), ("gn", gn)):
+            rowv[name] = sb.tile([P, PACK], F32, name=name + "_t")
+            nc.sync.dma_start(rowv[name][:], src.rearrange("(p t) o -> p (t o)", t=PACK))
+        hz_t = load_list("hz_t", hz)
+
+        picked_w = {}
+        dealt_w = {}
+        for name, offsets in (("a", ka_t), ("b", kb_t)):
+            picked_w[name] = sb.tile([P, H], U32, name="picked_w" + name, align_bytes=64)
+            gather_packed(picked_w[name][:], d_w, offsets)
+        xq_w = sb.tile([P, S], U32, name="xq_w", tag="xq_w", align_bytes=64)
+
+        def deal_words(name):
+            dealt_w[name] = sb.tile([P, H], U32, name="dealt_w" + name, align_bytes=64)
+            nc.vector.tensor_copy(
+                dealt_w[name][:].rearrange("p (t c i) -> p c t i", t=PACK, i=4),
+                picked_w[name][:].rearrange("p (c i t) -> p c t i", t=PACK, i=4),
+            )
+
+        dealt_scs = {}
+
+        def deal_scales(t):
+            dealt_scs[t] = sb.tile([P, 2 * P], U8, name="dealt_sc%d" % t, tag="dealt_sc%d" % t, align_bytes=64)
+            nc.vector.tensor_copy(dealt_scs[t][:], placed[:, 0 : 2 * H].rearrange("p (m t) -> p t m", t=PACK)[:, t, :])
+
+        deal_words("a")
+        gather_packed(xq_w[:], x_w, offs_t)
+        deal_scales(0)
+        deal_words("b")
+        deal_scales(1)
+
+        h_win = []
+
+        def make_h(t):
+            if t not in dealt_scs:
+                deal_scales(t)
+            dealt_sc = dealt_scs[t]
+            acc = psum.tile([P, S], F32, name="acc_h%d" % t, tag="acc_h%d" % t)
+            cols = slice(t * P, (t + 1) * P)
+            mx(acc[:], dealt_w["a"][:, cols], dealt_sc[:, 0:P], xq_w[:], placed[:, 2 * H :], True, False)
+            mx(acc[:], dealt_w["b"][:, cols], dealt_sc[:, P:], xq_w[:], placed[:, 2 * H :], False, True)
+            win = sb.tile([P, S], F32, name="h%d" % t)
+            if t == 0:
+                nc.scalar.activation(win[:], acc[:], ACT.Copy, scale=0.0625)
+            else:
+                nc.vector.tensor_scalar(win[:], acc[:], 0.0625, None, ALU.mult)
+            h_win.append(win)
+
+        pair = [sb.tile([P, 2, 2, W], F32, name="pair%d" % v) for v in range(2)]
+        ranked = [sb.tile([P, 2, 2, W], F32, name="ranked%d" % v) for v in range(2)]
+        ub = [sb.tile([P, 2 * S], F32, name="ub%d" % t) for t in range(PACK)]
+        sg = [sb.tile([P, 2, S], F32, name="sg%d" % v) for v in range(2)]
+        ug = [sb.tile([P, 2, S], F32, name="ug%d" % v) for v in range(2)]
+
+        def fetch_pairs(t):
+            nc.scalar.activation(pair[t // 2][:, 0, t % 2, :], h_win[t][:].indirect(n1_t[:]), ACT.Copy)
+            nc.scalar.activation(pair[t // 2][:, 1, t % 2, :], h_win[t][:].indirect(n2_t[:]), ACT.Copy)
+
+        def rank_pairs(v):
+            nc.vector.tensor_tensor(ranked[v][:, 0], pair[v][:, 0], pair[v][:, 1], ALU.max)
+            nc.vector.tensor_tensor(ranked[v][:, 1], pair[v][:, 0], pair[v][:, 1], ALU.min)
+
+        def put_larger(t):
+            nc.scalar.activation(ub[t][:].indirect(n3_t[:]), ranked[t // 2][:, 0, t % 2, :], ACT.Copy)
+
+        def put_smaller(t):
+            nc.scalar.activation(ub[t][:].indirect(n4_t[:]), ranked[t // 2][:, 1, t % 2, :], ACT.Copy)
+            nc.vector.tensor_scalar(ug[t // 2][:, t % 2, :], ub[t][:, 0:S], rowv["gn"][:, t : t + 1], None, ALU.mult)
+
+        z_in = [sb.tile([P, HALF, PACK], BF16, name="z_in%d" % u, align_bytes=64) for u in range(2)]
+        z_w = sb.tile([P, S], U32, name="z_w", align_bytes=64)
+        z_sc = sb.tile([P, S], U8, name="z_sc", align_bytes=64)
+        bias = sb.tile([P, PACK], F32, name="bias")
+
+        def gate(t, lo, hi):
+            nc.scalar.activation(
+                sg[t // 2][:, t % 2, lo:hi], ub[t][:].indirect(n5_t[:, lo // 16 : hi // 16]), ACT.Sigmoid,
+                scale=rowv["sl"][:, t : t + 1], bias=bias[:, t : t + 1],
+            )
+
+        def make_z(v, u):
+            cols = slice(u * HALF, (u + 1) * HALF)
+            nc.vector.tensor_tensor(
+                z_in[u][:, :, 2 * v : 2 * v + 2], ug[v][:, :, cols].rearrange("p t c -> p c t"),
+                sg[v][:, :, cols].rearrange("p t c -> p c t"), ALU.mult,
+            )
+
+        def quantise_z(u):
+            cols = slice(u * HALF, (u + 1) * HALF)
+            nc.vector.quantize_mx(z_w[:, cols].bitcast(FP8X4), z_sc[:, cols], z_in[u][:].rearrange("p c t -> p (c t)"))
+
+        for t in range(PACK):
+            make_h(t)
+            fetch_pairs(t)
+        nc.vector.scalar_tensor_tensor(bias[:], rowv["sl"][:], -1.0, rowv["th"][:], ALU.mult, ALU.mult)
+        rank_pairs(0)
+        rank_pairs(1)
+        put_larger(0)
+        put_larger(1)
+        put_smaller(0)
+        put_smaller(1)
+
+        for j, src in enumerate((w1_scales, w2_scales)):
+            for q in range(4):
+                nc.sync.dma_start(w_sc[32 * q : 32 * q + 4, j * N : (j + 1) * N].bitcast(I32), src[0, 4 * q : 4 * q + 4, :].bitcast(I32))
+        n8_t = load_list("n8_t", n8)
+        n9_t = load_list("n9_t", n9)
+        n6_t = load_list("n6_t", n6)
+        n7_t = load_list("n7_t", n7)
+        w2_w = load_words("w2_w", w2_words)
+        w1_w = load_words("w1_w", w1_words)
+        picked_hz = sb.tile([P, S], U8, name="picked_hz", tag="dealt_sc3", align_bytes=64)
+        gather_packed(picked_hz[:], x_sc, hz_t)
+        place_scale_rows(placed_hz, picked_hz, nc.sync)
+        xh_w = sb.tile([P, S], U32, name="xh_w", tag="xq_w", align_bytes=64)
+        gather_packed(xh_w[:], x_w, hz_t)
+        first = [psum.tile([P, HALF], F32, name="acc_first%d" % u, tag="acc_h%d" % u) for u in range(2)]
+        for u in range(2):
+            cols = slice(u * HALF, (u + 1) * HALF)
+            mx(first[u][:], w2_w[:, 0:P], w_sc[:, N : N + P], xh_w[:, cols], placed_hz[:, cols], True, False)
+        acc2 = {m: psum.tile([P, S], F32, name="acc_o%d" % m) for m in range(1, 4)}
+        for m in range(1, 4):
+            mx(acc2[m][:], w2_w[:, m * P : (m + 1) * P], w_sc[:, N + m * P : N + (m + 1) * P], xh_w[:], placed_hz[:], True, False)
+
+        gate(0, 0, S)
+        gate(1, 0, S)
+        put_larger(2)
+        put_larger(3)
+        make_z(0, 0)
+        make_z(0, 1)
+        put_smaller(2)
+        put_smaller(3)
+        for u in range(2):
+            gate(2, u * HALF, (u + 1) * HALF)
+            gate(3, u * HALF, (u + 1) * HALF)
+            make_z(1, u)
+        h2 = [sb.tile([P, S + 16], F32, name="h2_%d" % m) for m in range(4)]
+        for u in range(2):
+            quantise_z(u)
+            cols = slice(u * HALF, (u + 1) * HALF)
+            mx(first[u][:], w1_w[:, 0:P], w_sc[:, 0:P], z_w[:, cols], z_sc[:, cols], False, True)
+            nc.scalar.activation(h2[0][:, cols], first[u][:], ACT.Copy)
+        for m in range(1, 4):
+            mx(acc2[m][:], w1_w[:, m * P : (m + 1) * P], w_sc[:, m * P : (m + 1) * P], z_w[:], z_sc[:], False, True)
+            nc.vector.tensor_copy(h2[m][:, 0:S], acc2[m][:])
+
+        page, vals = {}, {}
+
+        def fetch_h2(m):
+            got = sb.tile([P, 2 * S], F32, name="got%d" % m)
+            nc.scalar.activation(got[:, 0:S], h2[m][:].indirect(n8_t[:]), ACT.Copy)
+            nc.scalar.activation(got[:, S:], h2[m][:].indirect(n9_t[:]), ACT.Copy)
+            vals[m] = sb.tile([P, 2 * S], F32, name="vals%d" % m)
+            nc.vector.tensor_tensor(vals[m][:, 0:S], h2[m][:, 0:S], got[:, 0:S], ALU.max)
+            nc.vector.tensor_tensor(vals[m][:, S:], h2[m][:, 0:S], got[:, S:], ALU.subtract)
+            page[m] = sb.tile([P, U], F32, name="page%d" % m)
+
+        def put_up(m):
+            nc.scalar.activation(page[m][:].indirect(n6_t[:]), vals[m][:, 0:S], ACT.Copy)
+
+        def put_dn(m):
+            nc.scalar.activation(page[m][:].indirect(n7_t[:]), vals[m][:, S:], ACT.Copy)
+            nc.sync.dma_start(out[m * P : (m + 1) * P, :], page[m][:])
+
+        for step in (fetch_h2, put_up, put_dn):
+            for m in range(4):
+                step(m)

@@ -54,7 +54,9 @@ def tile_picked_atznheordpagdd_none_p_kernel(
         def mx(acc, lw, ls, rw, rs, start, stop):
             nc.tensor.matmul_mx(acc, lhsT=lw.bitcast(FP8X4), lhsT_scale=ls, rhs=rw.bitcast(FP8X4), rhs_scale=rs, start=start, stop=stop)
 
-        d_sc = zeroed_bytes("d_sc", G)
+        d_sc = sb.tile([P, G], U8, name="d_sc", align_bytes=64)
+        nc.gpsimd.memset(d_sc[:, 0 : G // 2].bitcast(I32), 0)
+        nc.vector.memset(d_sc[:, G // 2 :].bitcast(I32), 0)
         x_sc = zeroed_bytes("x_sc", T)
         placed = zeroed_bytes("placed", 2 * H + S)
         placed_hz = zeroed_bytes("placed_hz", S)
@@ -71,7 +73,7 @@ def tile_picked_atznheordpagdd_none_p_kernel(
         d_w = load_words("d_w", d_words)
         x_w = load_words("x_w", x_words)
 
-        picked_sc = sb.tile([P, 2 * H + S], U8, name="picked_sc", align_bytes=64)
+        picked_sc = sb.tile([P, 2 * H + S], U8, name="picked_sc", tag="picked_sc", align_bytes=64)
         gather_packed(picked_sc[:, 0:H], d_sc, ka_t)
         gather_packed(picked_sc[:, H : 2 * H], d_sc, kb_t)
         gather_packed(picked_sc[:, 2 * H :], x_sc, offs_t)
@@ -95,11 +97,16 @@ def tile_picked_atznheordpagdd_none_p_kernel(
             gather_packed(picked_w[name][:], d_w, offsets)
         xq_w = sb.tile([P, S], U32, name="xq_w", tag="xq_w", align_bytes=64)
 
-        def deal_words(name):
-            dealt_w[name] = sb.tile([P, H], U32, name="dealt_w" + name, align_bytes=64)
+        dealt_first = sb.tile([P, 2 * P], U32, name="dealt_first", align_bytes=64)
+        dealt_rest = sb.tile([P, 6 * P], U32, name="dealt_rest", tag="picked_sc", align_bytes=64)
+        dealt_w["a", 0] = dealt_first[:]
+        for j, key in enumerate((("b", 0), ("a", 1), ("b", 1))):
+            dealt_w[key] = dealt_rest[:, 2 * P * j : 2 * P * (j + 1)]
+
+        def deal_words(name, v):
             nc.vector.tensor_copy(
-                dealt_w[name][:].rearrange("p (t c i) -> p c t i", t=PACK, i=4),
-                picked_w[name][:].rearrange("p (c i t) -> p c t i", t=PACK, i=4),
+                dealt_w[name, v].rearrange("p (t c i) -> p c t i", t=2, i=4),
+                picked_w[name][:].rearrange("p (c i t) -> p c t i", t=PACK, i=4)[:, :, 2 * v : 2 * v + 2, :],
             )
 
         dealt_scs = {}
@@ -108,32 +115,38 @@ def tile_picked_atznheordpagdd_none_p_kernel(
             dealt_scs[t] = sb.tile([P, 2 * P], U8, name="dealt_sc%d" % t, tag="dealt_sc%d" % t, align_bytes=64)
             nc.vector.tensor_copy(dealt_scs[t][:], placed[:, 0 : 2 * H].rearrange("p (m t) -> p t m", t=PACK)[:, t, :])
 
-        deal_words("a")
+        deal_words("a", 0)
         gather_packed(xq_w[:], x_w, offs_t)
         deal_scales(0)
-        deal_words("b")
+        deal_words("b", 0)
         deal_scales(1)
+        deal_words("a", 1)
+        deal_words("b", 1)
+        deal_scales(2)
+        deal_scales(3)
 
         h_win = []
 
         def make_h(t):
-            if t not in dealt_scs:
-                deal_scales(t)
             dealt_sc = dealt_scs[t]
-            acc = psum.tile([P, S], F32, name="acc_h%d" % t, tag="acc_h%d" % t)
-            cols = slice(t * P, (t + 1) * P)
-            mx(acc[:], dealt_w["a"][:, cols], dealt_sc[:, 0:P], xq_w[:], placed[:, 2 * H :], True, False)
-            mx(acc[:], dealt_w["b"][:, cols], dealt_sc[:, P:], xq_w[:], placed[:, 2 * H :], False, True)
+            rows = slice(t % 2 * P, (t % 2 + 1) * P)
             win = sb.tile([P, S], F32, name="h%d" % t)
-            if t == 0:
-                nc.scalar.activation(win[:], acc[:], ACT.Copy, scale=0.0625)
-            else:
-                nc.vector.tensor_scalar(win[:], acc[:], 0.0625, None, ALU.mult)
+            pieces = [(0, HALF), (HALF, S)] if t == 0 else [(0, S)]
+            accs = [psum.tile([P, hi - lo], F32, name="acc_h%d_%d" % (t, lo), tag="acc_h%d_%d" % (t, lo)) for lo, hi in pieces]
+            for name, first_col in (("a", 0), ("b", P)):
+                for acc, (lo, hi) in zip(accs, pieces):
+                    mx(acc[:], dealt_w[name, t // 2][:, rows], dealt_sc[:, first_col : first_col + P], xq_w[:, lo:hi],
+                       placed[:, 2 * H + lo : 2 * H + hi], name == "a", name == "b")
+            for acc, (lo, hi) in zip(accs, pieces):
+                if t == 0:
+                    nc.scalar.activation(win[:, lo:hi], acc[:], ACT.Copy, scale=0.0625)
+                else:
+                    nc.vector.tensor_scalar(win[:, lo:hi], acc[:], 0.0625, None, ALU.mult)
             h_win.append(win)
 
         pair = [sb.tile([P, 2, 2, W], F32, name="pair%d" % v) for v in range(2)]
         ranked = [sb.tile([P, 2, 2, W], F32, name="ranked%d" % v) for v in range(2)]
-        ub = [sb.tile([P, 2 * S], F32, name="ub%d" % t) for t in range(PACK)]
+        ub = [sb.tile([P, 2 * S if t < 2 else S], F32, name="ub%d" % t) for t in range(PACK)]
         sg = [sb.tile([P, 2, S], F32, name="sg%d" % v) for v in range(2)]
         ug = [sb.tile([P, 2, S], F32, name="ug%d" % v) for v in range(2)]
 
@@ -152,7 +165,8 @@ def tile_picked_atznheordpagdd_none_p_kernel(
             nc.scalar.activation(ub[t][:].indirect(n4_t[:]), ranked[t // 2][:, 1, t % 2, :], ACT.Copy)
             nc.vector.tensor_scalar(ug[t // 2][:, t % 2, :], ub[t][:, 0:S], rowv["gn"][:, t : t + 1], None, ALU.mult)
 
-        z_in = [sb.tile([P, HALF, PACK], BF16, name="z_in%d" % u, align_bytes=64) for u in range(2)]
+        z_pieces = [(0, HALF), (HALF, HALF + 64), (HALF + 64, S)]
+        z_in = [sb.tile([P, hi - lo, PACK], BF16, name="z_in%d" % lo, align_bytes=64) for lo, hi in z_pieces]
         z_w = sb.tile([P, S], U32, name="z_w", align_bytes=64)
         z_sc = sb.tile([P, S], U8, name="z_sc", align_bytes=64)
         bias = sb.tile([P, PACK], F32, name="bias")
@@ -164,24 +178,26 @@ def tile_picked_atznheordpagdd_none_p_kernel(
             )
 
         def make_z(v, u):
-            cols = slice(u * HALF, (u + 1) * HALF)
+            cols = slice(*z_pieces[u])
             nc.vector.tensor_tensor(
                 z_in[u][:, :, 2 * v : 2 * v + 2], ug[v][:, :, cols].rearrange("p t c -> p c t"),
                 sg[v][:, :, cols].rearrange("p t c -> p c t"), ALU.mult,
             )
 
         def quantise_z(u):
-            cols = slice(u * HALF, (u + 1) * HALF)
+            cols = slice(*z_pieces[u])
             nc.vector.quantize_mx(z_w[:, cols].bitcast(FP8X4), z_sc[:, cols], z_in[u][:].rearrange("p c t -> p (c t)"))
 
         for t in range(PACK):
             make_h(t)
+        for t in range(3):
             fetch_pairs(t)
-        nc.vector.scalar_tensor_tensor(bias[:], rowv["sl"][:], -1.0, rowv["th"][:], ALU.mult, ALU.mult)
         rank_pairs(0)
-        rank_pairs(1)
         put_larger(0)
         put_larger(1)
+        fetch_pairs(3)
+        nc.vector.scalar_tensor_tensor(bias[:], rowv["sl"][:], -1.0, rowv["th"][:], ALU.mult, ALU.mult)
+        rank_pairs(1)
         put_smaller(0)
         put_smaller(1)
 
@@ -199,7 +215,7 @@ def tile_picked_atznheordpagdd_none_p_kernel(
         place_scale_rows(placed_hz, picked_hz, nc.sync)
         xh_w = sb.tile([P, S], U32, name="xh_w", tag="xq_w", align_bytes=64)
         gather_packed(xh_w[:], x_w, hz_t)
-        first = [psum.tile([P, HALF], F32, name="acc_first%d" % u, tag="acc_h%d" % u) for u in range(2)]
+        first = [psum.tile([P, HALF], F32, name="acc_first%d" % u, tag="acc_h0_%d" % (u * HALF)) for u in range(2)]
         for u in range(2):
             cols = slice(u * HALF, (u + 1) * HALF)
             mx(first[u][:], w2_w[:, 0:P], w_sc[:, N : N + P], xh_w[:, cols], placed_hz[:, cols], True, False)
@@ -213,15 +229,17 @@ def tile_picked_atznheordpagdd_none_p_kernel(
         put_larger(3)
         make_z(0, 0)
         make_z(0, 1)
+        make_z(0, 2)
         put_smaller(2)
         put_smaller(3)
-        for u in range(2):
-            gate(2, u * HALF, (u + 1) * HALF)
-            gate(3, u * HALF, (u + 1) * HALF)
+        for u, (lo, hi) in enumerate(z_pieces):
+            gate(2, lo, hi)
+            gate(3, lo, hi)
             make_z(1, u)
         h2 = [sb.tile([P, S + 16], F32, name="h2_%d" % m) for m in range(4)]
-        for u in range(2):
+        for u in range(3):
             quantise_z(u)
+        for u in range(2):
             cols = slice(u * HALF, (u + 1) * HALF)
             mx(first[u][:], w1_w[:, 0:P], w_sc[:, 0:P], z_w[:, cols], z_sc[:, cols], False, True)
             nc.scalar.activation(h2[0][:, cols], first[u][:], ACT.Copy)

from contextlib import ExitStack

import concourse.mybir as mybir

K, T, S, N, G, H, W, U = 512, 1024, 256, 512, 2048, 512, 128, 512
FLOPS = 4 * 2 * 512 * 512 * 256

F32 = mybir.dt.float32
BF16 = mybir.dt.bfloat16
I32 = mybir.dt.int32
U32 = mybir.dt.uint32
U16 = mybir.dt.uint16
U8 = mybir.dt.uint8
FP8X4 = mybir.dt.float8_e4m3fn_x4
ALU = mybir.AluOpType
ACT = mybir.ActivationFunctionType
P = 128
PACK = 4
HALF = S // 2


def tile_picked_atznheordpagdd_none_p_kernel(
    tc, x_words, x_scales, d_words, d_scales, sl, th, gn, w1_words, w1_scales, w2_words, w2_scales,
    offs, ka, kb, n1, n2, n3, n4, n5, hz, n6, n7, n8, n9, out,
):
    nc = tc.nc
    with ExitStack() as ctx:
        lists = ctx.enter_context(tc.tile_pool(name="lists", bufs=1))
        sb = ctx.enter_context(tc.tile_pool(name="sb", bufs=1))
        psum = ctx.enter_context(tc.psum_pool(name="psum", bufs=1))

        def load_list(name, src):
            tile = lists.tile(list(src.shape), U16, name=name)
            nc.sync.dma_start(tile[:], src)
            return tile

        def load_words(name, src):
            tile = sb.tile([P, src.shape[2]], U32, name=name, align_bytes=64)
            nc.sync.dma_start(tile[:].bitcast(I32), src[0].rearrange("p n t -> p (n t)").bitcast(I32))
            return tile

        def zeroed_bytes(name, width):
            tile = sb.tile([P, width], U8, name=name, align_bytes=64)
            nc.vector.memset(tile[:].bitcast(I32), 0)
            return tile

        def gather_packed(dst, table, offsets):
            nc.vector.tensor_copy(dst, table[:].indirect(offsets[:]))

        def place_scale_rows(dst, src, queue):
            for a in range(4):
                queue.dma_start(dst[a:P:32, :].bitcast(I32), src[8 * a : P : 32, :].bitcast(I32))

        def mx(acc, lw, ls, rw, rs, start, stop):
            nc.tensor.matmul_mx(acc, lhsT=lw.bitcast(FP8X4), lhsT_scale=ls, rhs=rw.bitcast(FP8X4), rhs_scale=rs, start=start, stop=stop)

        d_sc = sb.tile([P, G], U8, name="d_sc", align_bytes=64)
        nc.gpsimd.memset(d_sc[:, 0 : G // 2].bitcast(I32), 0)
        nc.vector.memset(d_sc[:, G // 2 :].bitcast(I32), 0)
        x_sc = zeroed_bytes("x_sc", T)
        placed = zeroed_bytes("placed", 2 * H + S)
        placed_hz = zeroed_bytes("placed_hz", S)
        w_sc = zeroed_bytes("w_sc", 2 * N)

        warm = sb.tile([P, 2], F32, name="warm")
        nc.vector.memset(warm[:, 0:1], 0.0)
        nc.scalar.activation(warm[:, 1:2], warm[:, 0:1], ACT.Sigmoid)
        ka_t = load_list("ka_t", ka)
        nc.sync.dma_start(d_sc[0:P:8, :].bitcast(I32), d_scales[0].bitcast(I32))
        kb_t = load_list("kb_t", kb)
        offs_t = load_list("offs_t", offs)
        nc.sync.dma_start(x_sc[0:P:8, :].bitcast(I32), x_scales[0].bitcast(I32))
        d_w = load_words("d_w", d_words)
        x_w = load_words("x_w", x_words)

        picked_sc = sb.tile([P, 2 * H + S], U8, name="picked_sc", tag="picked_sc", align_bytes=64)
        gather_packed(picked_sc[:, 0:H], d_sc, ka_t)
        gather_packed(picked_sc[:, H : 2 * H], d_sc, kb_t)
        gather_packed(picked_sc[:, 2 * H :], x_sc, offs_t)
        place_scale_rows(placed, picked_sc, nc.scalar)

        n1_t = load_list("n1_t", n1)
        n2_t = load_list("n2_t", n2)
        n3_t = load_list("n3_t", n3)
        n4_t = load_list("n4_t", n4)
        n5_t = load_list("n5_t", n5)
        rowv = {}
        for name, src in (("sl", sl), ("th", th), ("gn", gn)):
            rowv[name] = sb.tile([P, PACK], F32, name=name + "_t")
            nc.sync.dma_start(rowv[name][:], src.rearrange("(p t) o -> p (t o)", t=PACK))
        hz_t = load_list("hz_t", hz)

        picked_w = {}
        dealt_w = {}
        for name, offsets in (("a", ka_t), ("b", kb_t)):
            picked_w[name] = sb.tile([P, H], U32, name="picked_w" + name, align_bytes=64)
            gather_packed(picked_w[name][:], d_w, offsets)
        xq_w = sb.tile([P, S], U32, name="xq_w", tag="xq_w", align_bytes=64)

        dealt_first = sb.tile([P, 2 * P], U32, name="dealt_first", align_bytes=64)
        dealt_rest = sb.tile([P, 6 * P], U32, name="dealt_rest", tag="picked_sc", align_bytes=64)
        dealt_w["a", 0] = dealt_first[:]
        for j, key in enumerate((("b", 0), ("a", 1), ("b", 1))):
            dealt_w[key] = dealt_rest[:, 2 * P * j : 2 * P * (j + 1)]

        def deal_words(name, v):
            nc.vector.tensor_copy(
                dealt_w[name, v].rearrange("p (t c i) -> p c t i", t=2, i=4),
                picked_w[name][:].rearrange("p (c i t) -> p c t i", t=PACK, i=4)[:, :, 2 * v : 2 * v + 2, :],
            )

        dealt_scs = {}

        def deal_scales(t):
            dealt_scs[t] = sb.tile([P, 2 * P], U8, name="dealt_sc%d" % t, tag="dealt_sc%d" % t, align_bytes=64)
            nc.vector.tensor_copy(dealt_scs[t][:], placed[:, 0 : 2 * H].rearrange("p (m t) -> p t m", t=PACK)[:, t, :])

        deal_words("a", 0)
        gather_packed(xq_w[:], x_w, offs_t)
        deal_scales(0)
        deal_words("b", 0)
        deal_scales(1)
        deal_words("a", 1)
        deal_words("b", 1)
        deal_scales(2)
        deal_scales(3)

        h_win = []

        def make_h(t):
            dealt_sc = dealt_scs[t]
            rows = slice(t % 2 * P, (t % 2 + 1) * P)
            win = sb.tile([P, S], F32, name="h%d" % t)
            pieces = [(0, HALF), (HALF, S)] if t == 0 else [(0, S)]
            accs = [psum.tile([P, hi - lo], F32, name="acc_h%d_%d" % (t, lo), tag="acc_h%d_%d" % (t, lo)) for lo, hi in pieces]
            for name, first_col in (("a", 0), ("b", P)):
                for acc, (lo, hi) in zip(accs, pieces):
                    mx(acc[:], dealt_w[name, t // 2][:, rows], dealt_sc[:, first_col : first_col + P], xq_w[:, lo:hi],
                       placed[:, 2 * H + lo : 2 * H + hi], name == "a", name == "b")
            for acc, (lo, hi) in zip(accs, pieces):
                if t == 0:
                    nc.scalar.activation(win[:, lo:hi], acc[:], ACT.Copy, scale=0.0625)
                else:
                    nc.vector.tensor_scalar(win[:, lo:hi], acc[:], 0.0625, None, ALU.mult)
            h_win.append(win)

        pair = [sb.tile([P, 2, 2, W], F32, name="pair%d" % v) for v in range(2)]
        ranked = [sb.tile([P, 2, 2, W], F32, name="ranked%d" % v) for v in range(2)]
        ub = [sb.tile([P, 2 * S if t < 2 else S], F32, name="ub%d" % t) for t in range(PACK)]
        sg = [sb.tile([P, 2, S], F32, name="sg%d" % v) for v in range(2)]
        ug = [sb.tile([P, 2, S], F32, name="ug%d" % v) for v in range(2)]

        def fetch_pairs(t):
            nc.scalar.activation(pair[t // 2][:, 0, t % 2, :], h_win[t][:].indirect(n1_t[:]), ACT.Copy)
            nc.scalar.activation(pair[t // 2][:, 1, t % 2, :], h_win[t][:].indirect(n2_t[:]), ACT.Copy)

        def rank_pairs(v):
            nc.vector.tensor_tensor(ranked[v][:, 0], pair[v][:, 0], pair[v][:, 1], ALU.max)
            nc.vector.tensor_tensor(ranked[v][:, 1], pair[v][:, 0], pair[v][:, 1], ALU.min)

        def put_larger(t):
            nc.scalar.activation(ub[t][:].indirect(n3_t[:]), ranked[t // 2][:, 0, t % 2, :], ACT.Copy)

        def put_smaller(t):
            nc.scalar.activation(ub[t][:].indirect(n4_t[:]), ranked[t // 2][:, 1, t % 2, :], ACT.Copy)
            nc.vector.tensor_scalar(ug[t // 2][:, t % 2, :], ub[t][:, 0:S], rowv["gn"][:, t : t + 1], None, ALU.mult)

        z_pieces = [(0, HALF), (HALF, HALF + 64), (HALF + 64, S)]
        z_in = [sb.tile([P, hi - lo, PACK], BF16, name="z_in%d" % lo, align_bytes=64) for lo, hi in z_pieces]
        z_w = sb.tile([P, S], U32, name="z_w", align_bytes=64)
        z_sc = sb.tile([P, S], U8, name="z_sc", align_bytes=64)
        bias = sb.tile([P, PACK], F32, name="bias")

        def gate(t, lo, hi):
            nc.scalar.activation(
                sg[t // 2][:, t % 2, lo:hi], ub[t][:].indirect(n5_t[:, lo // 16 : hi // 16]), ACT.Sigmoid,
                scale=rowv["sl"][:, t : t + 1], bias=bias[:, t : t + 1],
            )

        def make_z(v, u):
            cols = slice(*z_pieces[u])
            nc.vector.tensor_tensor(
                z_in[u][:, :, 2 * v : 2 * v + 2], ug[v][:, :, cols].rearrange("p t c -> p c t"),
                sg[v][:, :, cols].rearrange("p t c -> p c t"), ALU.mult,
            )

        def quantise_z(u):
            cols = slice(*z_pieces[u])
            nc.vector.quantize_mx(z_w[:, cols].bitcast(FP8X4), z_sc[:, cols], z_in[u][:].rearrange("p c t -> p (c t)"))

        for t in range(PACK):
            make_h(t)
        for t in range(3):
            fetch_pairs(t)
        rank_pairs(0)
        put_larger(0)
        put_larger(1)
        fetch_pairs(3)
        nc.vector.scalar_tensor_tensor(bias[:], rowv["sl"][:], -1.0, rowv["th"][:], ALU.mult, ALU.mult)
        rank_pairs(1)
        put_smaller(0)
        put_smaller(1)

        for j, src in enumerate((w1_scales, w2_scales)):
            for q in range(4):
                nc.sync.dma_start(w_sc[32 * q : 32 * q + 4, j * N : (j + 1) * N].bitcast(I32), src[0, 4 * q : 4 * q + 4, :].bitcast(I32))
        n8_t = load_list("n8_t", n8)
        n9_t = load_list("n9_t", n9)
        n6_t = load_list("n6_t", n6)
        n7_t = load_list("n7_t", n7)
        w2_w = load_words("w2_w", w2_words)
        w1_w = load_words("w1_w", w1_words)
        picked_hz = sb.tile([P, S], U8, name="picked_hz", tag="dealt_sc3", align_bytes=64)
        gather_packed(picked_hz[:], x_sc, hz_t)
        place_scale_rows(placed_hz, picked_hz, nc.sync)
        xh_w = sb.tile([P, S], U32, name="xh_w", tag="xq_w", align_bytes=64)
        gather_packed(xh_w[:], x_w, hz_t)
        first = [psum.tile([P, HALF], F32, name="acc_first%d" % u, tag="acc_h0_%d" % (u * HALF)) for u in range(2)]
        for u in range(2):
            cols = slice(u * HALF, (u + 1) * HALF)
            mx(first[u][:], w2_w[:, 0:P], w_sc[:, N : N + P], xh_w[:, cols], placed_hz[:, cols], True, False)
        acc2 = {m: psum.tile([P, S], F32, name="acc_o%d" % m) for m in range(1, 4)}
        for m in range(1, 4):
            mx(acc2[m][:], w2_w[:, m * P : (m + 1) * P], w_sc[:, N + m * P : N + (m + 1) * P], xh_w[:], placed_hz[:], True, False)

        gate(0, 0, S)
        gate(1, 0, S)
        put_larger(2)
        put_larger(3)
        make_z(0, 0)
        make_z(0, 1)
        make_z(0, 2)
        put_smaller(2)
        put_smaller(3)
        for u, (lo, hi) in enumerate(z_pieces):
            gate(2, lo, hi)
            gate(3, lo, hi)
            make_z(1, u)
        h2 = [sb.tile([P, S + 16], F32, name="h2_%d" % m) for m in range(4)]
        for u in range(3):
            quantise_z(u)
        for u in range(2):
            cols = slice(u * HALF, (u + 1) * HALF)
            mx(first[u][:], w1_w[:, 0:P], w_sc[:, 0:P], z_w[:, cols], z_sc[:, cols], False, True)
            nc.scalar.activation(h2[0][:, cols], first[u][:], ACT.Copy)
        for m in range(1, 4):
            mx(acc2[m][:], w1_w[:, m * P : (m + 1) * P], w_sc[:, m * P : (m + 1) * P], z_w[:], z_sc[:], False, True)
            nc.vector.tensor_copy(h2[m][:, 0:S], acc2[m][:])

        page, vals = {}, {}

        def fetch_h2(m):
            got = sb.tile([P, 2 * S], F32, name="got%d" % m)
            nc.scalar.activation(got[:, 0:S], h2[m][:].indirect(n8_t[:]), ACT.Copy)
            nc.scalar.activation(got[:, S:], h2[m][:].indirect(n9_t[:]), ACT.Copy)
            vals[m] = sb.tile([P, 2 * S], F32, name="vals%d" % m)
            nc.vector.tensor_tensor(vals[m][:, 0:S], h2[m][:, 0:S], got[:, 0:S], ALU.max)
            nc.vector.tensor_tensor(vals[m][:, S:], h2[m][:, 0:S], got[:, S:], ALU.subtract)
            page[m] = sb.tile([P, U], F32, name="page%d" % m)

        def put_up(m):
            nc.scalar.activation(page[m][:].indirect(n6_t[:]), vals[m][:, 0:S], ACT.Copy)

        def put_dn(m):
            nc.scalar.activation(page[m][:].indirect(n7_t[:]), vals[m][:, S:], ACT.Copy)
            nc.sync.dma_start(out[m * P : (m + 1) * P, :], page[m][:])

        for step in (fetch_h2, put_up, put_dn):
            for m in range(4):
                step(m)
